import numpy as np
import ml_dtypes


def mxq(x, axis, fmt="e4m3"):
    dtype, down = {"e4m3": (ml_dtypes.float8_e4m3fn, 7), "e5m2": (ml_dtypes.float8_e5m2, 14)}[fmt]
    v = np.moveaxis(np.asarray(x, np.float32).astype(ml_dtypes.bfloat16).astype(np.float64), axis, -1)
    blocks = v.reshape(v.shape[:-1] + (-1, 32))
    amax = np.abs(blocks).max(-1, keepdims=True)
    byte = np.maximum(np.where(amax > 0, np.frexp(amax)[1] - 1 + 127, 0) - down, 1)
    scale = np.exp2(byte - 127.0)
    codes = (blocks / scale).astype(np.float32).astype(dtype).astype(np.float64)
    return np.moveaxis((codes * scale).reshape(v.shape), -1, axis)


WIDE = False


def mx_kscale(k):
    if not WIDE:
        return np.ones(k)
    levels = np.array([10, -10, 5, -5, 0])
    if k % 512:
        return np.exp2(np.random.permutation(np.resize(levels, k // 32))).repeat(32)
    a = np.empty((k // 512, 16))
    for p in range(k // 512):
        a[p, :8] = np.random.permutation(np.resize(levels, 8))
        for g in range(8):
            far = levels[np.abs(levels - a[p, g]) >= 10]
            a[p, g + 8] = far[np.random.randint(len(far))]
    return np.exp2(a.ravel()).repeat(32)


BF16 = ml_dtypes.bfloat16


def bf(x):
    return np.asarray(x, np.float32).astype(BF16)


def f64(x):
    return np.asarray(x).astype(np.float64)


N, K, C = 384, 16, 512


def leaky(r):
    return np.maximum(r, 0.2 * r)


def neighbour_softmax(logits):
    m = np.max(logits, axis=1, keepdims=True)
    e = np.exp(logits - m)
    return e / np.sum(e, axis=1, keepdims=True)


def draw0():
    s, t = mx_kscale(C), mx_kscale(C)
    return {
        "xn": bf(np.random.standard_normal((N, K, C)) * s),
        "q": bf(np.random.standard_normal((N, C))),
        "delta": bf(np.random.standard_normal((N, K, C)) * 0.7),
        "wk": bf(np.random.standard_normal((C, C)) / np.sqrt(C) / s[:, None]),
        "wv": bf(np.random.standard_normal((C, C)) / np.sqrt(C) / s[:, None]),
        "gain": bf((1.0 + 0.1 * np.random.standard_normal(C)) * t),
        "wg": bf(1.5 * np.random.standard_normal((C, C)) / np.sqrt(C) / t[:, None]),
    }


def core(xn, q, delta, wk, wv, gain, wg):
    d = f64(delta)
    xq = mxq(f64(xn), 2, "e4m3")
    kx = xq @ mxq(f64(wk), 0, "e4m3")
    vx = xq @ mxq(f64(wv), 0, "e4m3")
    r = f64(q)[:, None, :] - kx + d
    h = leaky(r) * f64(gain)
    logits = mxq(h, 2, "e4m3") @ mxq(f64(wg), 0, "e4m3")
    a = neighbour_softmax(logits)
    return np.sum(a * (vx + d), axis=1)


def e4m3fn_bytes(y):
    return np.clip(np.asarray(y, np.float64), -448.0, 448.0).astype(np.float32).astype(ml_dtypes.float8_e4m3fn).view(np.uint8)


def e4m3fn_values(b):
    return np.asarray(b, np.uint8).view(ml_dtypes.float8_e4m3fn).astype(np.float64)


def setup_inputs():
    d = draw0()
    x0 = np.asarray(d['xn']).astype(np.float64)
    s = (np.max(np.abs(x0), axis=(0, 1), keepdims=True) / 448.0).astype(np.float32)
    out = {}
    for k, v in d.items():
        if k == 'xn':
            out['xn_bytes'] = e4m3fn_bytes(x0 / s.astype(np.float64))
            out['xn_scale'] = s
        else:
            out[k] = v
    return out


def reference(xn_bytes, xn_scale, q, delta, wk, wv, gain, wg):
    return core(e4m3fn_values(xn_bytes) * xn_scale.astype(np.float64), q, delta, wk, wv, gain, wg)

@@ -1,0 +1,370 @@
+from contextlib import ExitStack
+
+import concourse.mybir as mybir
+from concourse.masks import make_identity
+
+FLOPS = 3 * 2 * 384 * 16 * 512 * 512
+
+F32 = mybir.dt.float32
+BF16 = mybir.dt.bfloat16
+U32 = mybir.dt.uint32
+U8 = mybir.dt.uint8
+F8 = mybir.dt.float8_e4m3fn
+FP8X4 = mybir.dt.float8_e4m3fn_x4
+ALU = mybir.AluOpType
+ACT = mybir.ActivationFunctionType
+
+P = 128
+C = 512
+NB = 16
+BLOCKS = 3
+STEPS = 12
+JS = 4
+ROWS = JS * P
+EXP_PIECES = 4
+MUL_ENGINES = "GGGG"
+
+ORDER = [
+    ("L", 2, -4),
+    ("L", 3, -4),
+    ("W", 3, -4),
+    ("L", 0, -4),
+    ("L", 1, -4),
+    ("X", 0, 3),
+    ("R", 1, 0),
+    ("R", 0, 0),
+    ("R", 2, 0),
+    ("MAX", 0, -4),
+    ("R", 3, 0),
+    ("K", 0, 1),
+    ("K", 3, 1),
+    ("XQ", 0, 2),
+    ("SUM", 0, -5),
+    ("SUB", 3, -4),
+    ("SUB", 2, -4),
+    ("SUB", 1, -4),
+    ("H", 0, 0),
+    ("M", 1, -5),
+    ("SUB", 0, -4),
+    ("EXP", 3, -4),
+    ("OUT", 0, -6),
+    ("K", 1, 1),
+    ("K", 2, 1),
+    ("SUM", 1, -5),
+    ("XT", 0, 3),
+    ("XT", 1, 3),
+    ("EXP", 2, -4),
+    ("HQ", 0, 0),
+    ("M", 3, -4),
+    ("W", 2, -3),
+    ("M", 2, -4),
+    ("EXP", 1, -4),
+    ("EXP", 0, -4),
+    ("W", 0, -3),
+    ("W", 1, -4),
+    ("DIV", 0, -5),
+    ("M", 0, -4),
+]
+
+
+def tile_pointtransformervectorattention_t_kernel(
+    tc, xn_bytes, xn_scale, q, delta, wk, wv, gain, wg, out
+):
+    nc = tc.nc
+    with ExitStack() as ctx:
+        const = ctx.enter_context(tc.tile_pool(name="const", bufs=1))
+        wst = ctx.enter_context(tc.tile_pool(name="wst", bufs=2))
+        pool = ctx.enter_context(tc.tile_pool(name="pool", bufs=2))
+        psum = ctx.enter_context(tc.psum_pool(name="psum", bufs=1))
+
+        ident_f = const.tile([P, P], F32, name="ident_f")
+        ident_b = const.tile([P, P], BF16, name="ident_b")
+        scale4 = const.tile([P, JS, C], F32, name="scale4")
+        gcol = const.tile([P, 4], BF16, name="gcol")
+        sgn = const.tile([P, 4], F32, name="sgn")
+        gabs = const.tile([P, 4], F32, name="gabs")
+        warm = const.tile([P, 1], F32, name="warm")
+        qb = const.tile([P, BLOCKS, C], BF16, name="qb")
+        qf = const.tile([P, BLOCKS, 4, P], F32, name="qf")
+        wk_c = const.tile([P, C], U32, name="wk_c", align_bytes=64)
+        wv_c = const.tile([P, C], U32, name="wv_c", align_bytes=64)
+        wg_c = const.tile([P, C], U32, name="wg_c", align_bytes=64)
+        wk_s = const.tile([P, C], U8, name="wk_s", align_bytes=64)
+        wv_s = const.tile([P, C], U8, name="wv_s", align_bytes=64)
+        wg_s = const.tile([P, C], U8, name="wg_s", align_bytes=64)
+
+        xb, dt, xs, xg, xqc, xqs, nk, st, hg, hqc, hqs = {}, {}, {}, {}, {}, {}, {}, {}, {}, {}, {}
+        lps, lbs, ms, zs, ws, sgs, ots, wr = {}, {}, {}, {}, {}, {}, {}, {}
+
+        def once(store, key, make):
+            if key not in store:
+                store[key] = make()
+            return store[key]
+
+        def load_x(s):
+            if s < 0 or s >= STEPS or s in xb:
+                return
+            b, jg = divmod(s, 4)
+            t = pool.tile([P, JS * C], U8, name="xbytes", tag="xbytes", bufs=4)
+            nc.sync.dma_start(
+                out=t[:],
+                in_=xn_bytes[b * P : (b + 1) * P, jg * JS : (jg + 1) * JS, :].rearrange("p j c -> p (j c)"),
+            )
+            xb[s] = t
+
+        def load_d(s):
+            if s < 0 or s >= STEPS or s in dt:
+                return
+            b, jg = divmod(s, 4)
+            t = pool.tile([P, JS, C], BF16, name="dt", tag="dt", bufs=10)
+            nc.sync.dma_start(out=t[:], in_=delta[b * P : (b + 1) * P, jg * JS : (jg + 1) * JS, :])
+            dt[s] = t
+
+        def load_w(w):
+            t = wst.tile([P, 4, C], BF16, name="wraw", tag="wraw", bufs=2)
+            nc.sync.dma_start(out=t[:], in_=w.rearrange("(p j) n -> p j n", j=4))
+            return t
+
+        def quantize(codes, scales, src):
+            nc.vector.quantize_mx(out=codes[:].bitcast(FP8X4), scales=scales[:], in_=src)
+
+        def x_op(s, p):
+            t = pool.tile([P, JS * C], BF16, name="xs", tag="xs", bufs=2)
+            if s == 0:
+                for j in range(JS):
+                    cols = slice(j * C, (j + 1) * C)
+                    nc.vector.tensor_tensor(
+                        out=t[:, cols], in0=xb[0][:, cols].bitcast(F8), in1=scale4[:, 0, :], op=ALU.mult
+                    )
+                for j in range(1, JS):
+                    nc.vector.tensor_copy(out=scale4[:, j, :], in_=scale4[:, 0, :])
+            else:
+                nc.vector.tensor_tensor(
+                    out=t[:], in0=xb[s][:].bitcast(F8), in1=scale4[:].rearrange("p j c -> p (j c)"), op=ALU.mult
+                )
+            xs[s] = t
+            if s == 0:
+                g = wst.tile([P, C * 4], BF16, name="wgrp", tag="wgrp", bufs=1, align_bytes=64)
+                nc.vector.tensor_copy(
+                    out=g[:].rearrange("p (t m j) -> p t m j", t=4, j=4),
+                    in_=wr["k"][:].rearrange("p j (m t) -> p t m j", t=4),
+                )
+                wr["kg"] = g
+            if s == 1:
+                quantize(wk_c, wk_s, wr["kg"][:])
+                nc.vector.tensor_scalar(
+                    out=sgn[:], in0=gcol[:], scalar1=0.0, scalar2=2.0, op0=ALU.is_ge, op1=ALU.mult
+                )
+                for b in range(BLOCKS):
+                    nc.vector.tensor_copy(out=qf[:, b, :, :], in_=qb[:, b, :].rearrange("p (m t) -> p t m", t=4))
+                nc.vector.tensor_scalar_add(out=sgn[:], in0=sgn[:], scalar1=-1.0)
+                g = wst.tile([P, C * 4], BF16, name="wgrp", tag="wgrp", bufs=1, align_bytes=64)
+                nc.scalar.copy(
+                    out=g[:].rearrange("p (c j) -> p c j", j=4), in_=wr["v"][:].rearrange("p j c -> p c j")
+                )
+                wr["vg"] = g
+            if s == 2:
+                nc.vector.tensor_tensor(out=gabs[:], in0=gcol[:], in1=sgn[:], op=ALU.mult)
+                quantize(wv_c, wv_s, wr["vg"][:])
+                g = wst.tile([P, C * 4], BF16, name="wgrp", tag="wgrp", bufs=1, align_bytes=64)
+                nc.gpsimd.tensor_tensor(
+                    out=g[:].rearrange("p (c j) -> p c j", j=4),
+                    in0=wr["g"][:].rearrange("p j c -> p c j"),
+                    in1=sgn[:].unsqueeze(1).to_broadcast([P, C, 4]),
+                    op=ALU.mult,
+                )
+                wr["gg"] = g
+            if s == 3:
+                quantize(wg_c, wg_s, wr["gg"][:])
+
+        def xt_op(s, h):
+            g = once(xg, s, lambda: pool.tile([P, ROWS * 4], BF16, name="xg", tag="xg", bufs=2, align_bytes=64))
+            words = xs[s][:].bitcast(F32)
+            gw = g[:].bitcast(F32).rearrange("p (j r u) -> p j r u", j=JS, u=2)
+            xt = psum.tile([P, 2, 2, P], F32, name="wps", tag="wps", bufs=3)
+            for jj in range(2):
+                j = 2 * h + jj
+                for u in range(2):
+                    nc.tensor.transpose(xt[:, jj, u, :], words[:, j * 256 + u : (j + 1) * 256 : 2], ident_f[:])
+            nc.scalar.copy(out=gw[:, 2 * h : 2 * h + 2, :, :], in_=xt[:].rearrange("p j u r -> p j r u"))
+
+        def xq_op(s, p):
+            xqc[s] = pool.tile([P, ROWS], U32, name="xqc", tag="xqc", bufs=9, align_bytes=64)
+            xqs[s] = pool.tile([P, ROWS], U8, name="xqs", tag="xqs", bufs=9, align_bytes=64)
+            quantize(xqc[s], xqs[s], xg[s][:])
+
+        def k_op(s, j):
+            n = once(nk, s, lambda: pool.tile([P, JS, C], F32, name="nk", tag="nk", bufs=1))
+            kp = psum.tile([P, C], F32, name="wps", tag="wps", bufs=3)
+            cols = slice(j * P, (j + 1) * P)
+            nc.tensor.matmul_mx(
+                out=kp[:],
+                lhsT=xqc[s][:, cols].bitcast(FP8X4),
+                lhsT_scale=xqs[s][:, cols],
+                rhs=wk_c[:].bitcast(FP8X4),
+                rhs_scale=wk_s[:],
+                start=True,
+                stop=True,
+            )
+            nc.scalar.activation(out=n[:, j, :], in_=kp[:], func=ACT.Copy, scale=-1.0)
+
+        def r_op(s, t):
+            o = once(st, s, lambda: pool.tile([P, 4, ROWS], F32, name="st", tag="st", bufs=2))
+            rp = psum.tile([P, JS, P], F32, name="wps", tag="wps", bufs=3)
+            for j in range(JS):
+                d4 = dt[s][:, j, :].rearrange("p (m t) -> p t m", t=4)
+                nc.tensor.matmul(rp[:, j, :], lhsT=d4[:, t, :], rhs=ident_b[:], start=True, stop=False)
+                nc.tensor.matmul(
+                    rp[:, j, :],
+                    lhsT=nk[s][:, j, t * P : (t + 1) * P],
+                    rhs=ident_f[:],
+                    start=False,
+                    stop=False,
+                    is_transpose=True,
+                )
+                nc.tensor.matmul(
+                    rp[:, j, :], lhsT=qf[:, s // 4, t, :], rhs=ident_f[:], start=False, stop=True, is_transpose=True
+                )
+            nc.scalar.activation(
+                out=o[:, t, :], in_=rp[:].rearrange("p j r -> p (j r)"), func=ACT.Copy, scale=gabs[:, t : t + 1]
+            )
+
+        def h_op(s, p):
+            h = pool.tile([P, ROWS, 4], BF16, name="hg", tag="hg", bufs=2, align_bytes=64)
+            view = st[s][:].rearrange("p t r -> p r t")
+            nc.vector.scalar_tensor_tensor(out=h[:], in0=view, scalar=0.2, in1=view, op0=ALU.mult, op1=ALU.max)
+            hg[s] = h
+
+        def hq_op(s, p):
+            hqc[s] = pool.tile([P, ROWS], U32, name="hqc", tag="hqc", bufs=8, align_bytes=64)
+            hqs[s] = pool.tile([P, ROWS], U8, name="hqs", tag="hqs", bufs=8, align_bytes=64)
+            quantize(hqc[s], hqs[s], hg[s][:].rearrange("p r t -> p (r t)"))
+
+        def mx4(u, g, codes, scales, w_c, w_s, acc):
+            b, cb = divmod(u, 4)
+            s = 4 * b + g
+            for j in range(JS):
+                cols = slice(j * P, (j + 1) * P)
+                nc.tensor.matmul_mx(
+                    out=acc[:, j, :],
+                    lhsT=codes[s][:, cols].bitcast(FP8X4),
+                    lhsT_scale=scales[s][:, cols],
+                    rhs=w_c[:, cb * P : (cb + 1) * P].bitcast(FP8X4),
+                    rhs_scale=w_s[:, cb * P : (cb + 1) * P],
+                    start=True,
+                    stop=True,
+                )
+
+        def l_op(u, g):
+            lb = once(lbs, u, lambda: pool.tile([P, NB, P], BF16, name="lb", tag="lb", bufs=1))
+            lp = psum.tile([P, JS, P], F32, name="lps", tag="lps", bufs=4)
+            mx4(u, g, hqc, hqs, wg_c, wg_s, lp)
+            nc.scalar.copy(out=lb[:, g * JS : (g + 1) * JS, :], in_=lp[:])
+            lps[u, g] = lp
+
+        def max_op(u, p):
+            src, n = lbs[u], NB
+            while n > 1:
+                n = n // 2
+                dst = pool.tile([P, n, P], BF16, name="mx%d" % n, tag="mx%d" % n, bufs=2 if n == 1 else 1)
+                nc.vector.tensor_tensor(out=dst[:], in0=src[:, 0:n, :], in1=src[:, n : 2 * n, :], op=ALU.max)
+                src = dst
+            ms[u] = src
+
+        def sub_op(u, g):
+            z = once(zs, u, lambda: pool.tile([P, NB, P], F32, name="z", tag="z", bufs=2))
+            nc.vector.tensor_tensor(
+                out=z[:, g * JS : (g + 1) * JS, :],
+                in0=lps[u, g][:],
+                in1=ms[u][:].to_broadcast([P, JS, P]),
+                op=ALU.subtract,
+            )
+
+        def exp_op(u, p):
+            n = NB // EXP_PIECES
+            view = zs[u][:, p * n : (p + 1) * n, :]
+            nc.scalar.activation(out=view, in_=view, func=ACT.Exp)
+
+        def w_op(u, g):
+            b, cb = divmod(u, 4)
+            w = once(ws, u, lambda: pool.tile([P, NB, P], F32, name="w", tag="w", bufs=2))
+            vp = psum.tile([P, JS, P], F32, name="wps", tag="wps", bufs=3)
+            mx4(u, g, xqc, xqs, wv_c, wv_s, vp)
+            nc.vector.tensor_tensor(
+                out=w[:, g * JS : (g + 1) * JS, :],
+                in0=vp[:],
+                in1=dt[4 * b + g][:, :, cb * P : (cb + 1) * P],
+                op=ALU.add,
+            )
+
+        def m_op(u, p):
+            n = NB // len(MUL_ENGINES)
+            w = ws[u][:, p * n : (p + 1) * n, :]
+            e = zs[u][:, p * n : (p + 1) * n, :]
+            eng = nc.gpsimd if MUL_ENGINES[p] == "G" else nc.vector
+            eng.tensor_tensor(out=w, in0=w, in1=e, op=ALU.mult)
+
+        def sum_op(u, k):
+            sg = once(sgs, u, lambda: psum.tile([P, 2, P], F32, name="sg", tag="sg", bufs=1))
+            src = ws[u] if k else zs[u]
+            for j in range(NB):
+                nc.tensor.matmul(
+                    sg[:, k, :],
+                    lhsT=src[:, j, :],
+                    rhs=ident_f[:],
+                    start=(j == 0),
+                    stop=(j == NB - 1),
+                    is_transpose=True,
+                )
+
+        def div_op(u, p):
+            rd = pool.tile([P, P], F32, name="rd", tag="rd", bufs=1)
+            ot = pool.tile([P, P], F32, name="ot", tag="ot", bufs=2)
+            nc.vector.reciprocal(out=rd[:], in_=sgs[u][:, 0, :])
+            nc.vector.tensor_tensor(out=ot[:], in0=sgs[u][:, 1, :], in1=rd[:], op=ALU.mult)
+            ots[u] = ot
+
+        def out_op(u, p):
+            b, cb = divmod(u, 4)
+            op = psum.tile([P, P], F32, name="wps", tag="wps", bufs=3)
+            nc.tensor.transpose(op[:], ots[u][:], ident_f[:])
+            o = pool.tile([P, P], F32, name="o", tag="o", bufs=2)
+            nc.scalar.copy(out=o[:], in_=op[:])
+            nc.sync.dma_start(out=out[b * P : (b + 1) * P, cb * P : (cb + 1) * P], in_=o[:])
+
+        table = {
+            "X": x_op, "XT": xt_op, "XQ": xq_op, "K": k_op, "R": r_op, "H": h_op, "HQ": hq_op,
+            "L": l_op, "MAX": max_op, "SUB": sub_op, "EXP": exp_op, "W": w_op, "M": m_op,
+            "SUM": sum_op, "DIV": div_op, "OUT": out_op,
+        }
+
+        with tc.manual_schedule():
+            nc.vector.memset(warm[:], 0.0)
+            nc.scalar.dma_start(
+                out=scale4[:, 0, :], in_=xn_scale.rearrange("a b c -> (a b c)").partition_broadcast(P)
+            )
+            load_x(0)
+            wr["k"] = load_w(wk)
+            nc.sync.dma_start(out=gcol[:], in_=gain.rearrange("(p t) -> p t", t=4))
+            load_x(1)
+            nc.sync.dma_start(out=qb[:], in_=q.rearrange("(b p) c -> p b c", p=P))
+            load_d(0)
+            wr["v"] = load_w(wv)
+            make_identity(nc, ident_f[:])
+            make_identity(nc, ident_b[:])
+            nc.scalar.activation(out=warm[:], in_=warm[:], func=ACT.Exp)
+            load_x(2)
+            load_d(1)
+            load_x(3)
+
+            lo = min(off for name, p, off in ORDER)
+            hi = max(off for name, p, off in ORDER)
+            for i in range(-hi, STEPS - lo):
+                load_x(i + 3 + 2)
+                if i >= -1:
+                    load_d(i + 2)
+                if i == -1:
+                    wr["g"] = load_w(wg)
+                for name, p, off in ORDER:
+                    if 0 <= i + off < STEPS:
+                        table[name](i + off, p)

@@ -21,49 +21,56 @@ BLOCKS = 3
 STEPS = 12
 JS = 4
 ROWS = JS * P
-EXP_PIECES = 4
-MUL_ENGINES = "GGGG"
+HALF = 64
+EXP_PIECES = 2
+MUL_ENGINES = "GG"
 
 ORDER = [
-    ("L", 2, -4),
-    ("L", 3, -4),
-    ("W", 3, -4),
-    ("L", 0, -4),
     ("L", 1, -4),
-    ("X", 0, 3),
-    ("R", 1, 0),
-    ("R", 0, 0),
-    ("R", 2, 0),
-    ("MAX", 0, -4),
-    ("R", 3, 0),
-    ("K", 0, 1),
-    ("K", 3, 1),
+    ("L", 2, -4),
+    ("L", 0, -4),
+    ("W", 3, -4),
+    ("W", 0, -4),
+    ("L", 3, -4),
+    ("RD", 1, 0),
     ("XQ", 0, 2),
-    ("SUM", 0, -5),
-    ("SUB", 3, -4),
-    ("SUB", 2, -4),
+    ("RN", 1, 0),
+    ("MAX", 0, -4),
+    ("X", 0, 4),
+    ("MAX", 1, -4),
+    ("MAX", 2, -4),
+    ("RD", 2, 0),
+    ("RD", 3, 0),
+    ("RN", 2, 0),
+    ("RD", 0, 0),
+    ("RN", 3, 0),
+    ("MAX", 3, -4),
     ("SUB", 1, -4),
-    ("H", 0, 0),
-    ("M", 1, -5),
+    ("RN", 0, 0),
     ("SUB", 0, -4),
-    ("EXP", 3, -4),
-    ("OUT", 0, -6),
-    ("K", 1, 1),
+    ("SUM", 0, -5),
     ("K", 2, 1),
+    ("SUB", 2, -4),
+    ("K", 0, 1),
     ("SUM", 1, -5),
+    ("OUT", 0, -6),
+    ("K", 3, 1),
     ("XT", 0, 3),
-    ("XT", 1, 3),
-    ("EXP", 2, -4),
-    ("HQ", 0, 0),
-    ("M", 3, -4),
-    ("W", 2, -3),
-    ("M", 2, -4),
-    ("EXP", 1, -4),
+    ("SUB", 3, -4),
+    ("H", 0, 0),
+    ("K", 1, 1),
     ("EXP", 0, -4),
-    ("W", 0, -3),
+    ("M", 0, -5),
     ("W", 1, -4),
+    ("SUM", 2, -5),
+    ("XT", 1, 3),
+    ("HQ", 0, 0),
+    ("EXP", 1, -4),
+    ("SUM", 3, -5),
     ("DIV", 0, -5),
-    ("M", 0, -4),
+    ("W", 2, -3),
+    ("DIV", 1, -5),
+    ("M", 1, -4),
 ]
 
 
@@ -84,8 +91,7 @@ def tile_pointtransformervectorattention_t_kernel(
         sgn = const.tile([P, 4], F32, name="sgn")
         gabs = const.tile([P, 4], F32, name="gabs")
         warm = const.tile([P, 1], F32, name="warm")
-        qb = const.tile([P, BLOCKS, C], BF16, name="qb")
-        qf = const.tile([P, BLOCKS, 4, P], F32, name="qf")
+        fold = const.tile([P, HALF], BF16, name="fold")
         wk_c = const.tile([P, C], U32, name="wk_c", align_bytes=64)
         wv_c = const.tile([P, C], U32, name="wv_c", align_bytes=64)
         wg_c = const.tile([P, C], U32, name="wg_c", align_bytes=64)
@@ -93,6 +99,7 @@ def tile_pointtransformervectorattention_t_kernel(
         wv_s = const.tile([P, C], U8, name="wv_s", align_bytes=64)
         wg_s = const.tile([P, C], U8, name="wg_s", align_bytes=64)
 
+        dq, rps, rds = {}, {}, {}
         xb, dt, xs, xg, xqc, xqs, nk, st, hg, hqc, hqs = {}, {}, {}, {}, {}, {}, {}, {}, {}, {}, {}
         lps, lbs, ms, zs, ws, sgs, ots, wr = {}, {}, {}, {}, {}, {}, {}, {}
 
@@ -119,6 +126,22 @@ def tile_pointtransformervectorattention_t_kernel(
             t = pool.tile([P, JS, C], BF16, name="dt", tag="dt", bufs=10)
             nc.sync.dma_start(out=t[:], in_=delta[b * P : (b + 1) * P, jg * JS : (jg + 1) * JS, :])
             dt[s] = t
+
+        def load_dq(s):
+            if s < 0 or s >= STEPS or s in dq:
+                return
+            b, jg = divmod(s, 4)
+            t = pool.tile([P, 2, JS, C], BF16, name="dq", tag="dq", bufs=3)
+            nc.sync.dma_start(
+                out=t[0:HALF],
+                in_=delta[b * P : (b + 1) * P, jg * JS : (jg + 1) * JS, :].rearrange("(h p) j c -> p h j c", h=2),
+            )
+            for h in range(2):
+                r0 = b * P + h * HALF
+                nc.sync.dma_start(
+                    out=t[HALF:P, h, :, :], in_=q[r0 : r0 + HALF, :].unsqueeze(1).to_broadcast([HALF, JS, C])
+                )
+            dq[s] = t
 
         def load_w(w):
             t = wst.tile([P, 4, C], BF16, name="wraw", tag="wraw", bufs=2)
@@ -155,8 +178,6 @@ def tile_pointtransformervectorattention_t_kernel(
                 nc.vector.tensor_scalar(
                     out=sgn[:], in0=gcol[:], scalar1=0.0, scalar2=2.0, op0=ALU.is_ge, op1=ALU.mult
                 )
-                for b in range(BLOCKS):
-                    nc.vector.tensor_copy(out=qf[:, b, :, :], in_=qb[:, b, :].rearrange("p (m t) -> p t m", t=4))
                 nc.vector.tensor_scalar_add(out=sgn[:], in0=sgn[:], scalar1=-1.0)
                 g = wst.tile([P, C * 4], BF16, name="wgrp", tag="wgrp", bufs=1, align_bytes=64)
                 nc.scalar.copy(
@@ -208,22 +229,31 @@ def tile_pointtransformervectorattention_t_kernel(
             )
             nc.scalar.activation(out=n[:, j, :], in_=kp[:], func=ACT.Copy, scale=-1.0)
 
-        def r_op(s, t):
-            o = once(st, s, lambda: pool.tile([P, 4, ROWS], F32, name="st", tag="st", bufs=2))
+        def rd_op(s, t):
             rp = psum.tile([P, JS, P], F32, name="wps", tag="wps", bufs=3)
             for j in range(JS):
-                d4 = dt[s][:, j, :].rearrange("p (m t) -> p t m", t=4)
-                nc.tensor.matmul(rp[:, j, :], lhsT=d4[:, t, :], rhs=ident_b[:], start=True, stop=False)
+                for h in range(2):
+                    dq4 = dq[s][:, h, j, :].rearrange("p (m t) -> p t m", t=4)
+                    nc.tensor.matmul(
+                        rp[:, j, h * HALF : (h + 1) * HALF],
+                        lhsT=dq4[:, t, :],
+                        rhs=fold[:],
+                        start=(j == 0 and h == 0),
+                        stop=False,
+                    )
+            rps[s, t] = rp
+
+        def rn_op(s, t):
+            o = once(st, s, lambda: pool.tile([P, 4, ROWS], F32, name="st", tag="st", bufs=2))
+            rp = rps[s, t]
+            for j in range(JS):
                 nc.tensor.matmul(
                     rp[:, j, :],
                     lhsT=nk[s][:, j, t * P : (t + 1) * P],
                     rhs=ident_f[:],
                     start=False,
-                    stop=False,
+                    stop=(j == JS - 1),
                     is_transpose=True,
-                )
-                nc.tensor.matmul(
-                    rp[:, j, :], lhsT=qf[:, s // 4, t, :], rhs=ident_f[:], start=False, stop=True, is_transpose=True
                 )
             nc.scalar.activation(
                 out=o[:, t, :], in_=rp[:].rearrange("p j r -> p (j r)"), func=ACT.Copy, scale=gabs[:, t : t + 1]
@@ -263,13 +293,10 @@ def tile_pointtransformervectorattention_t_kernel(
             lps[u, g] = lp
 
         def max_op(u, p):
-            src, n = lbs[u], NB
-            while n > 1:
-                n = n // 2
-                dst = pool.tile([P, n, P], BF16, name="mx%d" % n, tag="mx%d" % n, bufs=2 if n == 1 else 1)
-                nc.vector.tensor_tensor(out=dst[:], in0=src[:, 0:n, :], in1=src[:, n : 2 * n, :], op=ALU.max)
-                src = dst
-            ms[u] = src
+            src, n = (ms[u] if p else lbs[u]), NB >> (p + 1)
+            dst = pool.tile([P, n, P], BF16, name="mx%d" % n, tag="mx%d" % n, bufs=2 if n == 1 else 1)
+            nc.vector.tensor_tensor(out=dst[:], in0=src[:, 0:n, :], in1=src[:, n : 2 * n, :], op=ALU.max)
+            ms[u] = dst
 
         def sub_op(u, g):
             z = once(zs, u, lambda: pool.tile([P, NB, P], F32, name="z", tag="z", bufs=2))
@@ -304,10 +331,11 @@ def tile_pointtransformervectorattention_t_kernel(
             eng = nc.gpsimd if MUL_ENGINES[p] == "G" else nc.vector
             eng.tensor_tensor(out=w, in0=w, in1=e, op=ALU.mult)
 
-        def sum_op(u, k):
+        def sum_op(u, p):
             sg = once(sgs, u, lambda: psum.tile([P, 2, P], F32, name="sg", tag="sg", bufs=1))
+            k, h = divmod(p, 2)
             src = ws[u] if k else zs[u]
-            for j in range(NB):
+            for j in range(8 * h, 8 * h + 8):
                 nc.tensor.matmul(
                     sg[:, k, :],
                     lhsT=src[:, j, :],
@@ -318,11 +346,14 @@ def tile_pointtransformervectorattention_t_kernel(
                 )
 
         def div_op(u, p):
-            rd = pool.tile([P, P], F32, name="rd", tag="rd", bufs=1)
-            ot = pool.tile([P, P], F32, name="ot", tag="ot", bufs=2)
-            nc.vector.reciprocal(out=rd[:], in_=sgs[u][:, 0, :])
-            nc.vector.tensor_tensor(out=ot[:], in0=sgs[u][:, 1, :], in1=rd[:], op=ALU.mult)
-            ots[u] = ot
+            if p == 0:
+                rd = pool.tile([P, P], F32, name="rd", tag="rd", bufs=1)
+                nc.vector.reciprocal(out=rd[:], in_=sgs[u][:, 0, :])
+                rds[u] = rd
+            else:
+                ot = pool.tile([P, P], F32, name="ot", tag="ot", bufs=2)
+                nc.vector.tensor_tensor(out=ot[:], in0=sgs[u][:, 1, :], in1=rds[u][:], op=ALU.mult)
+                ots[u] = ot
 
         def out_op(u, p):
             b, cb = divmod(u, 4)
@@ -333,7 +364,7 @@ def tile_pointtransformervectorattention_t_kernel(
             nc.sync.dma_start(out=out[b * P : (b + 1) * P, cb * P : (cb + 1) * P], in_=o[:])
 
         table = {
-            "X": x_op, "XT": xt_op, "XQ": xq_op, "K": k_op, "R": r_op, "H": h_op, "HQ": hq_op,
+            "X": x_op, "XT": xt_op, "XQ": xq_op, "K": k_op, "RD": rd_op, "RN": rn_op, "H": h_op, "HQ": hq_op,
             "L": l_op, "MAX": max_op, "SUB": sub_op, "EXP": exp_op, "W": w_op, "M": m_op,
             "SUM": sum_op, "DIV": div_op, "OUT": out_op,
         }
@@ -347,23 +378,23 @@ def tile_pointtransformervectorattention_t_kernel(
             wr["k"] = load_w(wk)
             nc.sync.dma_start(out=gcol[:], in_=gain.rearrange("(p t) -> p t", t=4))
             load_x(1)
-            nc.sync.dma_start(out=qb[:], in_=q.rearrange("(b p) c -> p b c", p=P))
-            load_d(0)
+            load_dq(0)
             wr["v"] = load_w(wv)
             make_identity(nc, ident_f[:])
             make_identity(nc, ident_b[:])
+            nc.gpsimd.tensor_tensor(out=fold[:], in0=ident_b[:, 0:HALF], in1=ident_b[:, HALF:P], op=ALU.add)
             nc.scalar.activation(out=warm[:], in_=warm[:], func=ACT.Exp)
             load_x(2)
-            load_d(1)
+            load_dq(1)
             load_x(3)
 
             lo = min(off for name, p, off in ORDER)
             hi = max(off for name, p, off in ORDER)
             for i in range(-hi, STEPS - lo):
-                load_x(i + 3 + 2)
-                if i >= -1:
-                    load_d(i + 2)
-                if i == -1:
+                load_x(i + 4 + 2)
+                load_dq(i + 0 + 2)
+                load_d(i + 1)
+                if i == -2:
                     wr["g"] = load_w(wg)
                 for name, p, off in ORDER:
                     if 0 <= i + off < STEPS:

@@ -22,55 +22,60 @@ STEPS = 12
 JS = 4
 ROWS = JS * P
 HALF = 64
-EXP_PIECES = 2
-MUL_ENGINES = "GG"
+EXP_PIECES = 4
+MUL_ENGINES = "GGGG"
 
 ORDER = [
-    ("L", 1, -4),
     ("L", 2, -4),
-    ("L", 0, -4),
-    ("W", 3, -4),
-    ("W", 0, -4),
-    ("L", 3, -4),
-    ("RD", 1, 0),
-    ("XQ", 0, 2),
-    ("RN", 1, 0),
-    ("MAX", 0, -4),
-    ("X", 0, 4),
-    ("MAX", 1, -4),
-    ("MAX", 2, -4),
-    ("RD", 2, 0),
-    ("RD", 3, 0),
-    ("RN", 2, 0),
-    ("RD", 0, 0),
-    ("RN", 3, 0),
-    ("MAX", 3, -4),
-    ("SUB", 1, -4),
-    ("RN", 0, 0),
-    ("SUB", 0, -4),
-    ("SUM", 0, -5),
-    ("K", 2, 1),
-    ("SUB", 2, -4),
-    ("K", 0, 1),
-    ("SUM", 1, -5),
-    ("OUT", 0, -6),
-    ("K", 3, 1),
-    ("XT", 0, 3),
-    ("SUB", 3, -4),
-    ("H", 0, 0),
-    ("K", 1, 1),
-    ("EXP", 0, -4),
-    ("M", 0, -5),
+    ("L", 1, -4),
     ("W", 1, -4),
+    ("L", 3, -4),
+    ("W", 3, -4),
+    ("L", 0, -4),
+    ("W", 0, -4),
+    ("MAX", 0, -4),
+    ("XQ", 0, 2),
+    ("RD", 0, 0),
+    ("MAX", 1, -4),
+    ("RD", 1, 0),
+    ("RN", 0, 0),
+    ("RN", 1, 0),
+    ("MAX", 2, -4),
+    ("RD", 3, 0),
+    ("X", 0, 5),
+    ("MAX", 3, -4),
+    ("RD", 2, 0),
+    ("SUM", 0, -5),
+    ("M", 3, -5),
+    ("H", 0, 0),
+    ("RN", 3, 0),
+    ("RN", 2, 0),
+    ("K", 1, 1),
+    ("SUM", 1, -5),
+    ("SUB", 2, -4),
+    ("SUB", 3, -4),
+    ("OUT", 0, -6),
+    ("M", 0, -5),
+    ("K", 2, 1),
+    ("H", 1, 0),
+    ("SUB", 1, -4),
+    ("K", 0, 1),
+    ("EXP", 2, -4),
+    ("SUB", 0, -4),
+    ("K", 3, 1),
     ("SUM", 2, -5),
-    ("XT", 1, 3),
+    ("EXP", 3, -4),
+    ("XT", 0, 4),
+    ("SUM", 3, -5),
     ("HQ", 0, 0),
     ("EXP", 1, -4),
-    ("SUM", 3, -5),
+    ("M", 2, -4),
     ("DIV", 0, -5),
+    ("EXP", 0, -4),
+    ("XT", 1, 4),
+    ("M", 1, -4),
     ("W", 2, -3),
     ("DIV", 1, -5),
-    ("M", 1, -4),
 ]
 
 
@@ -260,10 +265,11 @@ def tile_pointtransformervectorattention_t_kernel(
             )
 
         def h_op(s, p):
-            h = pool.tile([P, ROWS, 4], BF16, name="hg", tag="hg", bufs=2, align_bytes=64)
-            view = st[s][:].rearrange("p t r -> p r t")
-            nc.vector.scalar_tensor_tensor(out=h[:], in0=view, scalar=0.2, in1=view, op0=ALU.mult, op1=ALU.max)
-            hg[s] = h
+            h = once(hg, s, lambda: pool.tile([P, ROWS, 4], BF16, name="hg", tag="hg", bufs=2, align_bytes=64))
+            view = st[s][:, 2 * p : 2 * p + 2, :].rearrange("p t r -> p r t")
+            nc.vector.scalar_tensor_tensor(
+                out=h[:, :, 2 * p : 2 * p + 2], in0=view, scalar=0.2, in1=view, op0=ALU.mult, op1=ALU.max
+            )
 
         def hq_op(s, p):
             hqc[s] = pool.tile([P, ROWS], U32, name="hqc", tag="hqc", bufs=8, align_bytes=64)
@@ -391,10 +397,10 @@ def tile_pointtransformervectorattention_t_kernel(
             lo = min(off for name, p, off in ORDER)
             hi = max(off for name, p, off in ORDER)
             for i in range(-hi, STEPS - lo):
-                load_x(i + 4 + 2)
+                load_x(i + 5 + 2)
                 load_dq(i + 0 + 2)
                 load_d(i + 1)
-                if i == -2:
+                if i == -3:
                     wr["g"] = load_w(wg)
                 for name, p, off in ORDER:
                     if 0 <= i + off < STEPS:

from contextlib import ExitStack

import concourse.mybir as mybir
from concourse.masks import make_identity

FLOPS = 3 * 2 * 384 * 16 * 512 * 512

F32 = mybir.dt.float32
BF16 = mybir.dt.bfloat16
U32 = mybir.dt.uint32
U8 = mybir.dt.uint8
F8 = mybir.dt.float8_e4m3fn
FP8X4 = mybir.dt.float8_e4m3fn_x4
ALU = mybir.AluOpType
ACT = mybir.ActivationFunctionType

P = 128
C = 512
NB = 16
BLOCKS = 3
STEPS = 12
JS = 4
ROWS = JS * P
HALF = 64
EXP_PIECES = 4
MUL_ENGINES = "GGGG"

ORDER = [
    ("L", 2, -4),
    ("L", 1, -4),
    ("W", 1, -4),
    ("L", 3, -4),
    ("W", 3, -4),
    ("L", 0, -4),
    ("W", 0, -4),
    ("MAX", 0, -4),
    ("XQ", 0, 2),
    ("RD", 0, 0),
    ("MAX", 1, -4),
    ("RD", 1, 0),
    ("RN", 0, 0),
    ("RN", 1, 0),
    ("MAX", 2, -4),
    ("RD", 3, 0),
    ("X", 0, 5),
    ("MAX", 3, -4),
    ("RD", 2, 0),
    ("SUM", 0, -5),
    ("M", 3, -5),
    ("H", 0, 0),
    ("RN", 3, 0),
    ("RN", 2, 0),
    ("K", 1, 1),
    ("SUM", 1, -5),
    ("SUB", 2, -4),
    ("SUB", 3, -4),
    ("OUT", 0, -6),
    ("M", 0, -5),
    ("K", 2, 1),
    ("H", 1, 0),
    ("SUB", 1, -4),
    ("K", 0, 1),
    ("EXP", 2, -4),
    ("SUB", 0, -4),
    ("K", 3, 1),
    ("SUM", 2, -5),
    ("EXP", 3, -4),
    ("XT", 0, 4),
    ("SUM", 3, -5),
    ("HQ", 0, 0),
    ("EXP", 1, -4),
    ("M", 2, -4),
    ("DIV", 0, -5),
    ("EXP", 0, -4),
    ("XT", 1, 4),
    ("M", 1, -4),
    ("W", 2, -3),
    ("DIV", 1, -5),
]


def tile_pointtransformervectorattention_t_kernel(
    tc, xn_bytes, xn_scale, q, delta, wk, wv, gain, wg, out
):
    nc = tc.nc
    with ExitStack() as ctx:
        const = ctx.enter_context(tc.tile_pool(name="const", bufs=1))
        wst = ctx.enter_context(tc.tile_pool(name="wst", bufs=2))
        pool = ctx.enter_context(tc.tile_pool(name="pool", bufs=2))
        psum = ctx.enter_context(tc.psum_pool(name="psum", bufs=1))

        ident_f = const.tile([P, P], F32, name="ident_f")
        ident_b = const.tile([P, P], BF16, name="ident_b")
        scale4 = const.tile([P, JS, C], F32, name="scale4")
        gcol = const.tile([P, 4], BF16, name="gcol")
        sgn = const.tile([P, 4], F32, name="sgn")
        gabs = const.tile([P, 4], F32, name="gabs")
        warm = const.tile([P, 1], F32, name="warm")
        fold = const.tile([P, HALF], BF16, name="fold")
        wk_c = const.tile([P, C], U32, name="wk_c", align_bytes=64)
        wv_c = const.tile([P, C], U32, name="wv_c", align_bytes=64)
        wg_c = const.tile([P, C], U32, name="wg_c", align_bytes=64)
        wk_s = const.tile([P, C], U8, name="wk_s", align_bytes=64)
        wv_s = const.tile([P, C], U8, name="wv_s", align_bytes=64)
        wg_s = const.tile([P, C], U8, name="wg_s", align_bytes=64)

        dq, rps, rds = {}, {}, {}
        xb, dt, xs, xg, xqc, xqs, nk, st, hg, hqc, hqs = {}, {}, {}, {}, {}, {}, {}, {}, {}, {}, {}
        lps, lbs, ms, zs, ws, sgs, ots, wr = {}, {}, {}, {}, {}, {}, {}, {}

        def once(store, key, make):
            if key not in store:
                store[key] = make()
            return store[key]

        def load_x(s):
            if s < 0 or s >= STEPS or s in xb:
                return
            b, jg = divmod(s, 4)
            t = pool.tile([P, JS * C], U8, name="xbytes", tag="xbytes", bufs=4)
            nc.sync.dma_start(
                out=t[:],
                in_=xn_bytes[b * P : (b + 1) * P, jg * JS : (jg + 1) * JS, :].rearrange("p j c -> p (j c)"),
            )
            xb[s] = t

        def load_d(s):
            if s < 0 or s >= STEPS or s in dt:
                return
            b, jg = divmod(s, 4)
            t = pool.tile([P, JS, C], BF16, name="dt", tag="dt", bufs=10)
            nc.sync.dma_start(out=t[:], in_=delta[b * P : (b + 1) * P, jg * JS : (jg + 1) * JS, :])
            dt[s] = t

        def load_dq(s):
            if s < 0 or s >= STEPS or s in dq:
                return
            b, jg = divmod(s, 4)
            t = pool.tile([P, 2, JS, C], BF16, name="dq", tag="dq", bufs=3)
            nc.sync.dma_start(
                out=t[0:HALF],
                in_=delta[b * P : (b + 1) * P, jg * JS : (jg + 1) * JS, :].rearrange("(h p) j c -> p h j c", h=2),
            )
            for h in range(2):
                r0 = b * P + h * HALF
                nc.sync.dma_start(
                    out=t[HALF:P, h, :, :], in_=q[r0 : r0 + HALF, :].unsqueeze(1).to_broadcast([HALF, JS, C])
                )
            dq[s] = t

        def load_w(w):
            t = wst.tile([P, 4, C], BF16, name="wraw", tag="wraw", bufs=2)
            nc.sync.dma_start(out=t[:], in_=w.rearrange("(p j) n -> p j n", j=4))
            return t

        def quantize(codes, scales, src):
            nc.vector.quantize_mx(out=codes[:].bitcast(FP8X4), scales=scales[:], in_=src)

        def x_op(s, p):
            t = pool.tile([P, JS * C], BF16, name="xs", tag="xs", bufs=2)
            if s == 0:
                for j in range(JS):
                    cols = slice(j * C, (j + 1) * C)
                    nc.vector.tensor_tensor(
                        out=t[:, cols], in0=xb[0][:, cols].bitcast(F8), in1=scale4[:, 0, :], op=ALU.mult
                    )
                for j in range(1, JS):
                    nc.vector.tensor_copy(out=scale4[:, j, :], in_=scale4[:, 0, :])
            else:
                nc.vector.tensor_tensor(
                    out=t[:], in0=xb[s][:].bitcast(F8), in1=scale4[:].rearrange("p j c -> p (j c)"), op=ALU.mult
                )
            xs[s] = t
            if s == 0:
                g = wst.tile([P, C * 4], BF16, name="wgrp", tag="wgrp", bufs=1, align_bytes=64)
                nc.vector.tensor_copy(
                    out=g[:].rearrange("p (t m j) -> p t m j", t=4, j=4),
                    in_=wr["k"][:].rearrange("p j (m t) -> p t m j", t=4),
                )
                wr["kg"] = g
            if s == 1:
                quantize(wk_c, wk_s, wr["kg"][:])
                nc.vector.tensor_scalar(
                    out=sgn[:], in0=gcol[:], scalar1=0.0, scalar2=2.0, op0=ALU.is_ge, op1=ALU.mult
                )
                nc.vector.tensor_scalar_add(out=sgn[:], in0=sgn[:], scalar1=-1.0)
                g = wst.tile([P, C * 4], BF16, name="wgrp", tag="wgrp", bufs=1, align_bytes=64)
                nc.scalar.copy(
                    out=g[:].rearrange("p (c j) -> p c j", j=4), in_=wr["v"][:].rearrange("p j c -> p c j")
                )
                wr["vg"] = g
            if s == 2:
                nc.vector.tensor_tensor(out=gabs[:], in0=gcol[:], in1=sgn[:], op=ALU.mult)
                quantize(wv_c, wv_s, wr["vg"][:])
                g = wst.tile([P, C * 4], BF16, name="wgrp", tag="wgrp", bufs=1, align_bytes=64)
                nc.gpsimd.tensor_tensor(
                    out=g[:].rearrange("p (c j) -> p c j", j=4),
                    in0=wr["g"][:].rearrange("p j c -> p c j"),
                    in1=sgn[:].unsqueeze(1).to_broadcast([P, C, 4]),
                    op=ALU.mult,
                )
                wr["gg"] = g
            if s == 3:
                quantize(wg_c, wg_s, wr["gg"][:])

        def xt_op(s, h):
            g = once(xg, s, lambda: pool.tile([P, ROWS * 4], BF16, name="xg", tag="xg", bufs=2, align_bytes=64))
            words = xs[s][:].bitcast(F32)
            gw = g[:].bitcast(F32).rearrange("p (j r u) -> p j r u", j=JS, u=2)
            xt = psum.tile([P, 2, 2, P], F32, name="wps", tag="wps", bufs=3)
            for jj in range(2):
                j = 2 * h + jj
                for u in range(2):
                    nc.tensor.transpose(xt[:, jj, u, :], words[:, j * 256 + u : (j + 1) * 256 : 2], ident_f[:])
            nc.scalar.copy(out=gw[:, 2 * h : 2 * h + 2, :, :], in_=xt[:].rearrange("p j u r -> p j r u"))

        def xq_op(s, p):
            xqc[s] = pool.tile([P, ROWS], U32, name="xqc", tag="xqc", bufs=9, align_bytes=64)
            xqs[s] = pool.tile([P, ROWS], U8, name="xqs", tag="xqs", bufs=9, align_bytes=64)
            quantize(xqc[s], xqs[s], xg[s][:])

        def k_op(s, j):
            n = once(nk, s, lambda: pool.tile([P, JS, C], F32, name="nk", tag="nk", bufs=1))
            kp = psum.tile([P, C], F32, name="wps", tag="wps", bufs=3)
            cols = slice(j * P, (j + 1) * P)
            nc.tensor.matmul_mx(
                out=kp[:],
                lhsT=xqc[s][:, cols].bitcast(FP8X4),
                lhsT_scale=xqs[s][:, cols],
                rhs=wk_c[:].bitcast(FP8X4),
                rhs_scale=wk_s[:],
                start=True,
                stop=True,
            )
            nc.scalar.activation(out=n[:, j, :], in_=kp[:], func=ACT.Copy, scale=-1.0)

        def rd_op(s, t):
            rp = psum.tile([P, JS, P], F32, name="wps", tag="wps", bufs=3)
            for j in range(JS):
                for h in range(2):
                    dq4 = dq[s][:, h, j, :].rearrange("p (m t) -> p t m", t=4)
                    nc.tensor.matmul(
                        rp[:, j, h * HALF : (h + 1) * HALF],
                        lhsT=dq4[:, t, :],
                        rhs=fold[:],
                        start=(j == 0 and h == 0),
                        stop=False,
                    )
            rps[s, t] = rp

        def rn_op(s, t):
            o = once(st, s, lambda: pool.tile([P, 4, ROWS], F32, name="st", tag="st", bufs=2))
            rp = rps[s, t]
            for j in range(JS):
                nc.tensor.matmul(
                    rp[:, j, :],
                    lhsT=nk[s][:, j, t * P : (t + 1) * P],
                    rhs=ident_f[:],
                    start=False,
                    stop=(j == JS - 1),
                    is_transpose=True,
                )
            nc.scalar.activation(
                out=o[:, t, :], in_=rp[:].rearrange("p j r -> p (j r)"), func=ACT.Copy, scale=gabs[:, t : t + 1]
            )

        def h_op(s, p):
            h = once(hg, s, lambda: pool.tile([P, ROWS, 4], BF16, name="hg", tag="hg", bufs=2, align_bytes=64))
            view = st[s][:, 2 * p : 2 * p + 2, :].rearrange("p t r -> p r t")
            nc.vector.scalar_tensor_tensor(
                out=h[:, :, 2 * p : 2 * p + 2], in0=view, scalar=0.2, in1=view, op0=ALU.mult, op1=ALU.max
            )

        def hq_op(s, p):
            hqc[s] = pool.tile([P, ROWS], U32, name="hqc", tag="hqc", bufs=8, align_bytes=64)
            hqs[s] = pool.tile([P, ROWS], U8, name="hqs", tag="hqs", bufs=8, align_bytes=64)
            quantize(hqc[s], hqs[s], hg[s][:].rearrange("p r t -> p (r t)"))

        def mx4(u, g, codes, scales, w_c, w_s, acc):
            b, cb = divmod(u, 4)
            s = 4 * b + g
            for j in range(JS):
                cols = slice(j * P, (j + 1) * P)
                nc.tensor.matmul_mx(
                    out=acc[:, j, :],
                    lhsT=codes[s][:, cols].bitcast(FP8X4),
                    lhsT_scale=scales[s][:, cols],
                    rhs=w_c[:, cb * P : (cb + 1) * P].bitcast(FP8X4),
                    rhs_scale=w_s[:, cb * P : (cb + 1) * P],
                    start=True,
                    stop=True,
                )

        def l_op(u, g):
            lb = once(lbs, u, lambda: pool.tile([P, NB, P], BF16, name="lb", tag="lb", bufs=1))
            lp = psum.tile([P, JS, P], F32, name="lps", tag="lps", bufs=4)
            mx4(u, g, hqc, hqs, wg_c, wg_s, lp)
            nc.scalar.copy(out=lb[:, g * JS : (g + 1) * JS, :], in_=lp[:])
            lps[u, g] = lp

        def max_op(u, p):
            src, n = (ms[u] if p else lbs[u]), NB >> (p + 1)
            dst = pool.tile([P, n, P], BF16, name="mx%d" % n, tag="mx%d" % n, bufs=2 if n == 1 else 1)
            nc.vector.tensor_tensor(out=dst[:], in0=src[:, 0:n, :], in1=src[:, n : 2 * n, :], op=ALU.max)
            ms[u] = dst

        def sub_op(u, g):
            z = once(zs, u, lambda: pool.tile([P, NB, P], F32, name="z", tag="z", bufs=2))
            nc.vector.tensor_tensor(
                out=z[:, g * JS : (g + 1) * JS, :],
                in0=lps[u, g][:],
                in1=ms[u][:].to_broadcast([P, JS, P]),
                op=ALU.subtract,
            )

        def exp_op(u, p):
            n = NB // EXP_PIECES
            view = zs[u][:, p * n : (p + 1) * n, :]
            nc.scalar.activation(out=view, in_=view, func=ACT.Exp)

        def w_op(u, g):
            b, cb = divmod(u, 4)
            w = once(ws, u, lambda: pool.tile([P, NB, P], F32, name="w", tag="w", bufs=2))
            vp = psum.tile([P, JS, P], F32, name="wps", tag="wps", bufs=3)
            mx4(u, g, xqc, xqs, wv_c, wv_s, vp)
            nc.vector.tensor_tensor(
                out=w[:, g * JS : (g + 1) * JS, :],
                in0=vp[:],
                in1=dt[4 * b + g][:, :, cb * P : (cb + 1) * P],
                op=ALU.add,
            )

        def m_op(u, p):
            n = NB // len(MUL_ENGINES)
            w = ws[u][:, p * n : (p + 1) * n, :]
            e = zs[u][:, p * n : (p + 1) * n, :]
            eng = nc.gpsimd if MUL_ENGINES[p] == "G" else nc.vector
            eng.tensor_tensor(out=w, in0=w, in1=e, op=ALU.mult)

        def sum_op(u, p):
            sg = once(sgs, u, lambda: psum.tile([P, 2, P], F32, name="sg", tag="sg", bufs=1))
            k, h = divmod(p, 2)
            src = ws[u] if k else zs[u]
            for j in range(8 * h, 8 * h + 8):
                nc.tensor.matmul(
                    sg[:, k, :],
                    lhsT=src[:, j, :],
                    rhs=ident_f[:],
                    start=(j == 0),
                    stop=(j == NB - 1),
                    is_transpose=True,
                )

        def div_op(u, p):
            if p == 0:
                rd = pool.tile([P, P], F32, name="rd", tag="rd", bufs=1)
                nc.vector.reciprocal(out=rd[:], in_=sgs[u][:, 0, :])
                rds[u] = rd
            else:
                ot = pool.tile([P, P], F32, name="ot", tag="ot", bufs=2)
                nc.vector.tensor_tensor(out=ot[:], in0=sgs[u][:, 1, :], in1=rds[u][:], op=ALU.mult)
                ots[u] = ot

        def out_op(u, p):
            b, cb = divmod(u, 4)
            op = psum.tile([P, P], F32, name="wps", tag="wps", bufs=3)
            nc.tensor.transpose(op[:], ots[u][:], ident_f[:])
            o = pool.tile([P, P], F32, name="o", tag="o", bufs=2)
            nc.scalar.copy(out=o[:], in_=op[:])
            nc.sync.dma_start(out=out[b * P : (b + 1) * P, cb * P : (cb + 1) * P], in_=o[:])

        table = {
            "X": x_op, "XT": xt_op, "XQ": xq_op, "K": k_op, "RD": rd_op, "RN": rn_op, "H": h_op, "HQ": hq_op,
            "L": l_op, "MAX": max_op, "SUB": sub_op, "EXP": exp_op, "W": w_op, "M": m_op,
            "SUM": sum_op, "DIV": div_op, "OUT": out_op,
        }

        with tc.manual_schedule():
            nc.vector.memset(warm[:], 0.0)
            nc.scalar.dma_start(
                out=scale4[:, 0, :], in_=xn_scale.rearrange("a b c -> (a b c)").partition_broadcast(P)
            )
            load_x(0)
            wr["k"] = load_w(wk)
            nc.sync.dma_start(out=gcol[:], in_=gain.rearrange("(p t) -> p t", t=4))
            load_x(1)
            load_dq(0)
            wr["v"] = load_w(wv)
            make_identity(nc, ident_f[:])
            make_identity(nc, ident_b[:])
            nc.gpsimd.tensor_tensor(out=fold[:], in0=ident_b[:, 0:HALF], in1=ident_b[:, HALF:P], op=ALU.add)
            nc.scalar.activation(out=warm[:], in_=warm[:], func=ACT.Exp)
            load_x(2)
            load_dq(1)
            load_x(3)

            lo = min(off for name, p, off in ORDER)
            hi = max(off for name, p, off in ORDER)
            for i in range(-hi, STEPS - lo):
                load_x(i + 5 + 2)
                load_dq(i + 0 + 2)
                load_d(i + 1)
                if i == -3:
                    wr["g"] = load_w(wg)
                for name, p, off in ORDER:
                    if 0 <= i + off < STEPS:
                        table[name](i + off, p)
